import numpy as np
import ml_dtypes


def mxq(x, axis, fmt="e4m3"):
    dtype, down = {"e4m3": (ml_dtypes.float8_e4m3fn, 7), "e5m2": (ml_dtypes.float8_e5m2, 14)}[fmt]
    v = np.moveaxis(np.asarray(x, np.float32).astype(ml_dtypes.bfloat16).astype(np.float64), axis, -1)
    blocks = v.reshape(v.shape[:-1] + (-1, 32))
    amax = np.abs(blocks).max(-1, keepdims=True)
    byte = np.maximum(np.where(amax > 0, np.frexp(amax)[1] - 1 + 127, 0) - down, 1)
    scale = np.exp2(byte - 127.0)
    codes = (blocks / scale).astype(np.float32).astype(dtype).astype(np.float64)
    return np.moveaxis((codes * scale).reshape(v.shape), -1, axis)


WIDE = False


def mx_kscale(k):
    if not WIDE:
        return np.ones(k)
    levels = np.array([10, -10, 5, -5, 0])
    if k % 512:
        return np.exp2(np.random.permutation(np.resize(levels, k // 32))).repeat(32)
    a = np.empty((k // 512, 16))
    for p in range(k // 512):
        a[p, :8] = np.random.permutation(np.resize(levels, 8))
        for g in range(8):
            far = levels[np.abs(levels - a[p, g]) >= 10]
            a[p, g + 8] = far[np.random.randint(len(far))]
    return np.exp2(a.ravel()).repeat(32)


def f64(x):
    return np.asarray(x).astype(np.float64)


def striped(idx):
    return np.tile(idx.reshape(-1, 16).T, (8, 1)).astype(np.uint16)


def unstriped(offs):
    return offs[:16].T.reshape(-1).astype(np.int64)


E2M1 = np.array([0.0, 0.5, 1.0, 1.5, 2.0, 3.0, 4.0, 6.0, -0.0, -0.5, -1.0, -1.5, -2.0, -3.0, -4.0, -6.0])


def pack_weight(w, fmt):
    k, n = w.shape
    w = f64(np.asarray(w, np.float32).astype(ml_dtypes.bfloat16)).reshape(k // 32, 32, n)
    amax = np.abs(w).max(1)
    if fmt == "e4m3":
        byte = np.frexp(amax)[1] - 1 + 127 - 7
    else:
        mant, ex = np.frexp(amax / 6.0)
        byte = np.where(mant > 0.5, ex, ex - 1) + 127
    byte = np.clip(np.where(amax > 0, byte, 1), 1, 254)
    scaled = (w * np.exp2(127.0 - byte)[:, None, :]).reshape(k, n).astype(np.float32)
    by_word = np.ascontiguousarray(scaled.reshape(k // 512, 128, 4, n).transpose(0, 1, 3, 2))
    if fmt == "e4m3":
        words = by_word.astype(ml_dtypes.float8_e4m3fn).view(np.uint8)
    else:
        c = by_word.astype(ml_dtypes.float4_e2m1fn).view(np.uint8) & 0xF
        words = (c[..., 0::2] | (c[..., 1::2] << 4)).reshape(k // 512, 128, 2 * n)
    return np.ascontiguousarray(words), np.ascontiguousarray(byte.astype(np.uint8).reshape(k // 512, 16, n))


def unpack_weight(words, scales, fmt):
    g, _, n = scales.shape
    words = np.ascontiguousarray(words).reshape(g, 128, n, -1)
    if fmt == "e4m3":
        vals = words.view(ml_dtypes.float8_e4m3fn).astype(np.float64)
    else:
        nib = np.empty((g, 128, n, 4), np.uint8)
        nib[..., 0::2] = words & 0xF
        nib[..., 1::2] = words >> 4
        vals = E2M1[nib]
    vals = vals * np.repeat(np.exp2(scales.astype(np.float64) - 127.0), 8, axis=1)[..., None]
    return vals.transpose(0, 1, 3, 2).reshape(g * 512, n)


def d_relu(v):
    return (v > 0).astype(np.float64)


K, T, E, C, H, N = 256, 1024, 8, 256, 512, 512


def by_expert(wq, xq):
    return np.concatenate([wq[e].T @ xq[:, e * C:(e + 1) * C] for e in range(E)], axis=1)


def setup_inputs():
    n = np.random.standard_normal
    s = mx_kscale(N)[:, None]
    u = mx_kscale(H)
    first = np.random.permutation(np.repeat(np.arange(E), T // E))
    second = (first + 1 + np.random.permutation(np.repeat(np.arange(E - 1), -(-T // (E - 1)))[:T])) % E
    while np.bincount(second, minlength=E).max() != T // E:
        load = np.bincount(second, minlength=E); hi, lo = int(load.argmax()), int(load.argmin())
        t = np.flatnonzero((second == hi) & (first != lo))[0]; second[t] = lo
    slot_token = np.empty(E * C, np.int64); pos = np.empty((2, T), np.int64); fill = np.zeros(E, np.int64)
    place = np.stack([np.random.permutation(C) for _ in range(E)])
    for r, deal in enumerate((first, second)):
        for t in np.random.permutation(T):
            e = deal[t]; j = e * C + place[e, fill[e]]; fill[e] += 1; slot_token[j] = t; pos[r, t] = j
    g = np.random.uniform(0.2, 0.8, T)
    w_slot = np.empty(E * C); w_slot[pos[0]] = g; w_slot[pos[1]] = 1.0 - g
    w2 = [pack_weight(m, "e2m1") for m in n((E, N, H)) / np.sqrt(N) / s[None] * u[None, None, :]]
    w1 = [pack_weight(m, "e2m1") for m in n((E, H, K)) / np.sqrt(H) / u[None, :, None]]
    return {
        "dyT": (n((N, T)) * s).astype(np.float32),
        "a": n((H, E * C)).astype(np.float32),
        "w2_words": np.stack([m[0] for m in w2]),
        "w2_scales": np.stack([m[1] for m in w2]),
        "w1_words": np.stack([m[0] for m in w1]),
        "w1_scales": np.stack([m[1] for m in w1]),
        "gate": np.tile(w_slot, (N, 1)).astype(np.float32),
        "offs": striped(slot_token),
        "pos1": striped(pos[0]),
        "pos2": striped(pos[1]),
    }


def reference(dyT, a, w2_words, w2_scales, w1_words, w1_scales, gate, offs, pos1, pos2):
    idx = unstriped(offs)
    w2 = np.stack([unpack_weight(w2_words[e], w2_scales[e], "e2m1") for e in range(E)])
    w1 = np.stack([unpack_weight(w1_words[e], w1_scales[e], "e2m1") for e in range(E)])
    gq = mxq(f64(gate) * f64(dyT)[:, idx], 0, "e4m3")
    dh = by_expert(w2, gq)
    da = dh * d_relu(f64(a))
    dx = by_expert(w1, mxq(da, 0, "e4m3"))
    return dx[:, unstriped(pos1)] + dx[:, unstriped(pos2)]

@@ -1,0 +1,229 @@
+from contextlib import ExitStack
+
+import concourse.mybir as mybir
+
+K, T, E, C, H, N = 256, 1024, 8, 256, 512, 512
+S = E * C
+P = 128
+PACK = 4
+
+F32 = mybir.dt.float32
+BF16 = mybir.dt.bfloat16
+I32 = mybir.dt.int32
+U32 = mybir.dt.uint32
+U16 = mybir.dt.uint16
+U8 = mybir.dt.uint8
+FP8X4 = mybir.dt.float8_e4m3fn_x4
+FP4X4 = mybir.dt.float4_e2m1fn_x4
+MULT = mybir.AluOpType.mult
+ADD = mybir.AluOpType.add
+MAX = mybir.AluOpType.max
+SIGN = mybir.ActivationFunctionType.Sign
+
+FLOPS = 2 * S * (N * H + H * K)
+BYTES = 4 * N * T + 4 * H * S + E * (N * H + H * K) * 17 // 32 + 4 * S + 2 * S + 2 * 2 * T + 4 * K * T
+
+PIECE = 512
+PIECES = S // PIECE
+CHUNK = 128
+SHARES = (((0, 512, "gpsimd"), (512, 512, "gpsimd")), ((0, 512, "gpsimd"), (512, 256, "gpsimd"), (768, 256, "vector")))
+
+
+def tile_moe_bdx_mlp_relu_kernel(
+    tc, dyT, a, w2_words, w2_scales, w1_words, w1_scales, gate, offs, pos1, pos2, out
+):
+    nc = tc.nc
+    with ExitStack() as ctx:
+        lists = ctx.enter_context(tc.tile_pool(name="lists", bufs=1))
+        keep = ctx.enter_context(tc.tile_pool(name="keep", bufs=1))
+        work = ctx.enter_context(tc.tile_pool(name="work", bufs=4))
+        psum1 = ctx.enter_context(tc.psum_pool(name="psum1", bufs=4))
+        psum2 = ctx.enter_context(tc.psum_pool(name="psum2", bufs=2))
+
+        offs_t = lists.tile([P, S // 16], U16, name="offs_t")
+        pos1_t = lists.tile([P, T // 16], U16, name="pos1_t")
+        pos2_t = lists.tile([P, T // 16], U16, name="pos2_t")
+
+        dy = [keep.tile([P, T], F32, name=f"dy{t}") for t in range(PACK)]
+        gates = [keep.tile([P, PIECE], F32, name=f"gates{q}") for q in range(PIECES)]
+        pre = [keep.tile([P, PACK, PIECE], F32, name=f"pre{q}") for q in range(PIECES)]
+        w2_raw = [keep.tile([P, 2, 2 * H], U8, name=f"w2_raw{q}") for q in range(PIECES)]
+        w2_t = [keep.tile([P, 2, 2 * H], U8, name=f"w2_t{q}", align_bytes=64) for q in range(PIECES)]
+        s2_raw = keep.tile([P, E, H], U8, name="s2_raw")
+        s2_t = [keep.tile([P, 2, H], U8, name=f"s2_t{q}", align_bytes=64) for q in range(PIECES)]
+        w1_t = [keep.tile([P, 2, 2 * K], U8, name=f"w1_t{q}", align_bytes=64) for q in range(PIECES)]
+        s1_t = keep.tile([P, E, K], U8, name="s1_t", align_bytes=64)
+        dx = [keep.tile([P, S], F32, name=f"dx{k}") for k in range(2)]
+
+        nc.vector.memset(s2_raw[:].rearrange("p e i -> p (e i)").bitcast(I32), 0)
+        nc.gpsimd.memset(s1_t[:].rearrange("p e i -> p (e i)").bitcast(I32), 0)
+
+        dyT_rows = dyT.rearrange("(p t) n -> p t n", t=PACK)
+        a_rows = a.rearrange("(p t) s -> p t s", t=PACK)
+
+        def load_gate(q):
+            nc.sync.dma_start(gates[q][:], gate[0:P, q * PIECE : (q + 1) * PIECE])
+
+        def load_pre(q):
+            nc.sync.dma_start(pre[q][:], a_rows[:, :, q * PIECE : (q + 1) * PIECE])
+
+        def load_w2(q):
+            nc.sync.dma_start(
+                w2_raw[q][:].rearrange("p e b -> p (e b)").bitcast(I32).rearrange("p (e b) -> p e b", e=2),
+                w2_words[2 * q : 2 * q + 2].rearrange("e g p b -> p (e g) b").bitcast(I32),
+            )
+
+        def load_w1(q):
+            nc.sync.dma_start(
+                w1_t[q][:].rearrange("p e b -> p (e b)").bitcast(I32).rearrange("p (e b) -> p e b", e=2),
+                w1_words[2 * q : 2 * q + 2].rearrange("e g p b -> p (e g) b").bitcast(I32),
+            )
+
+        def load_scales(tile, scales):
+            for quad in range(4):
+                nc.sync.dma_start(
+                    tile[32 * quad : 32 * quad + 4].rearrange("p e i -> p (e i)").bitcast(I32).rearrange("p (e i) -> p e i", e=E),
+                    scales[:, :, 4 * quad : 4 * quad + 4, :].rearrange("e g f i -> f (e g) i").bitcast(I32),
+                )
+
+        nc.sync.dma_start(offs_t[:], offs)
+        load_gate(0)
+        for t in range(PACK):
+            nc.sync.dma_start(dy[t][:], dyT_rows[:, t, :])
+        load_scales(s2_raw, w2_scales)
+        load_w2(0)
+        load_pre(0)
+        load_gate(1)
+        load_scales(s1_t, w1_scales)
+        load_w1(0)
+        for q in range(1, PIECES):
+            load_w2(q)
+            load_pre(q)
+            load_w1(q)
+            if q + 1 < PIECES:
+                load_gate(q + 1)
+        nc.sync.dma_start(pos1_t[:], pos1)
+        nc.sync.dma_start(pos2_t[:], pos2)
+
+        g4 = {}
+        codes = {}
+        signs = {}
+
+        def gather(q, t):
+            if t == 0:
+                g4[q] = work.tile([P, PACK, PIECE], F32, name="g4")
+            nc.vector.tensor_tensor(
+                g4[q][:, t, :],
+                dy[t][:].indirect(offs_t[:, q * (PIECE // 16) : (q + 1) * (PIECE // 16)]),
+                gates[q][:],
+                MULT,
+            )
+
+        def permute(q):
+            nc.vector.tensor_copy(
+                w2_t[q][:].rearrange("p e b -> p (e b)").bitcast(U16).rearrange("p (e t m) -> p e t m", e=2, t=PACK),
+                w2_raw[q][:].rearrange("p e b -> p (e b)").bitcast(U16).rearrange("p (e m t) -> p e t m", e=2, t=PACK),
+            )
+            nc.vector.tensor_copy(
+                s2_t[q][:].rearrange("p e (t m) -> p e t m", t=PACK),
+                s2_raw[:, 2 * q : 2 * q + 2, :].rearrange("p e (m t) -> p e t m", t=PACK),
+            )
+
+        def interleave(e):
+            q, h = divmod(e, 2)
+            gb = work.tile([P, C, PACK], BF16, name="gb", align_bytes=64)
+            nc.scalar.copy(gb[:], g4[q][:, :, h * C : (h + 1) * C].rearrange("p t s -> p s t"))
+            return gb
+
+        def sign(e):
+            q, h = divmod(e, 2)
+            sg = work.tile([P, C, PACK], BF16, name="sg")
+            nc.scalar.activation(sg[:], pre[q][:, :, h * C : (h + 1) * C].rearrange("p t s -> p s t"), SIGN)
+            signs[e] = sg
+
+        def quantise_g(e):
+            words = work.tile([P, C], U32, name="g_words", align_bytes=64)
+            scales = work.tile([P, C], U8, name="g_scales", align_bytes=64)
+            nc.vector.quantize_mx(
+                out=words[:].bitcast(FP8X4), scales=scales[:], in_=grouped[e][:].rearrange("p s t -> p (s t)")
+            )
+            codes[e] = words, scales
+
+        def first_product(e, c):
+            q, h = divmod(e, 2)
+            words, scales = codes[e]
+            if c == 0:
+                das[e] = work.tile([P, C, PACK], BF16, name="da", align_bytes=64)
+            cols = slice(c * CHUNK, (c + 1) * CHUNK)
+            bank = psum1.tile([P, PACK, CHUNK], F32, name="bank")
+            for t in range(PACK):
+                nc.tensor.matmul_mx(
+                    out=bank[:, t, :],
+                    lhsT=w2_t[q][:, h, t * 2 * P : (t + 1) * 2 * P].bitcast(FP4X4),
+                    lhsT_scale=s2_t[q][:, h, t * P : (t + 1) * P],
+                    rhs=words[:, cols].bitcast(FP8X4),
+                    rhs_scale=scales[:, cols],
+                    start=True,
+                    stop=True,
+                )
+            nc.vector.scalar_tensor_tensor(
+                das[e][:, cols, :], signs[e][:, cols, :], 0.0, bank[:].rearrange("p t s -> p s t"), MAX, MULT
+            )
+
+        def second_product(e, first, width):
+            q, h = divmod(e, 2)
+            words = work.tile([P, C], U32, name="da_words", align_bytes=64)
+            scales = work.tile([P, C], U8, name="da_scales", align_bytes=64)
+            nc.vector.quantize_mx(
+                out=words[:, 0:width].bitcast(FP8X4),
+                scales=scales[:, 0:width],
+                in_=das[e][:, first : first + width, :].rearrange("p s t -> p (s t)"),
+            )
+            for k in range(2):
+                acc = psum2.tile([P, C], F32, name=f"acc{k}")
+                nc.tensor.matmul_mx(
+                    out=acc[:, 0:width],
+                    lhsT=w1_t[q][:, h, k * 2 * P : (k + 1) * 2 * P].bitcast(FP4X4),
+                    lhsT_scale=s1_t[:, e, k * P : (k + 1) * P],
+                    rhs=words[:, 0:width].bitcast(FP8X4),
+                    rhs_scale=scales[:, 0:width],
+                    start=True,
+                    stop=True,
+                )
+                nc.scalar.copy(dx[k][:, e * C + first : e * C + first + width], acc[:, 0:width])
+
+        grouped = {}
+        das = {}
+
+        def fetch(q):
+            for t in range(PACK):
+                gather(q, t)
+            for e in (2 * q, 2 * q + 1):
+                grouped[e] = interleave(e)
+                sign(e)
+
+        fetch(0)
+        permute(0)
+        for q in range(PIECES):
+            if q + 1 < PIECES:
+                fetch(q + 1)
+                permute(q + 1)
+            for e in (2 * q, 2 * q + 1):
+                quantise_g(e)
+                first_product(e, 0)
+                if e > 0:
+                    second_product(e - 1, 0, C)
+                first_product(e, 1)
+        second_product(E - 1, 0, CHUNK)
+        second_product(E - 1, CHUNK, CHUNK)
+
+        for k in range(2):
+            part1 = keep.tile([P, T], F32, name=f"part1_{k}")
+            nc.vector.tensor_copy(part1[:], dx[k][:].indirect(pos1_t[:]))
+            for first, width, adder in SHARES[k]:
+                part2 = keep.tile([P, width], F32, name=f"part2_{k}_{first}")
+                total = keep.tile([P, width], F32, name=f"total_{k}_{first}")
+                nc.vector.tensor_copy(part2[:], dx[k][:].indirect(pos2_t[:, first // 16 : (first + width) // 16]))
+                engine = nc.vector if adder == "vector" else nc.gpsimd
+                engine.tensor_tensor(total[:], part1[:, first : first + width], part2[:], ADD)
+                nc.sync.dma_start(out[k * P : (k + 1) * P, first : first + width], total[:])

@@ -19,6 +19,7 @@ MULT = mybir.AluOpType.mult
 ADD = mybir.AluOpType.add
 MAX = mybir.AluOpType.max
 SIGN = mybir.ActivationFunctionType.Sign
+RELU = mybir.ActivationFunctionType.Relu
 
 FLOPS = 2 * S * (N * H + H * K)
 BYTES = 4 * N * T + 4 * H * S + E * (N * H + H * K) * 17 // 32 + 4 * S + 2 * S + 2 * 2 * T + 4 * K * T
@@ -36,7 +37,7 @@ def tile_moe_bdx_mlp_relu_kernel(
     with ExitStack() as ctx:
         lists = ctx.enter_context(tc.tile_pool(name="lists", bufs=1))
         keep = ctx.enter_context(tc.tile_pool(name="keep", bufs=1))
-        work = ctx.enter_context(tc.tile_pool(name="work", bufs=4))
+        work = ctx.enter_context(tc.tile_pool(name="work", bufs=3))
         psum1 = ctx.enter_context(tc.psum_pool(name="psum1", bufs=4))
         psum2 = ctx.enter_context(tc.psum_pool(name="psum2", bufs=2))
 
@@ -49,13 +50,16 @@ def tile_moe_bdx_mlp_relu_kernel(
         pre = [keep.tile([P, PACK, PIECE], F32, name=f"pre{q}") for q in range(PIECES)]
         w2_raw = [keep.tile([P, 2, 2 * H], U8, name=f"w2_raw{q}") for q in range(PIECES)]
         w2_t = [keep.tile([P, 2, 2 * H], U8, name=f"w2_t{q}", align_bytes=64) for q in range(PIECES)]
-        s2_raw = keep.tile([P, E, H], U8, name="s2_raw")
-        s2_t = [keep.tile([P, 2, H], U8, name=f"s2_t{q}", align_bytes=64) for q in range(PIECES)]
-        w1_t = [keep.tile([P, 2, 2 * K], U8, name=f"w1_t{q}", align_bytes=64) for q in range(PIECES)]
+        s2_raw = keep.tile([P, E // 2, H], U8, name="s2_raw")
+        s2_mid = keep.tile([P, E // 2, H], U8, name="s2_mid")
+        s2_t = keep.tile([P, E, H], U8, name="s2_t", align_bytes=64)
+        w1_t = keep.tile([P, E, 2 * K], U8, name="w1_t", align_bytes=64)
         s1_t = keep.tile([P, E, K], U8, name="s1_t", align_bytes=64)
         dx = [keep.tile([P, S], F32, name=f"dx{k}") for k in range(2)]
 
-        nc.vector.memset(s2_raw[:].rearrange("p e i -> p (e i)").bitcast(I32), 0)
+        for rows in (slice(32, 64), slice(64, P)):
+            nc.gpsimd.memset(s2_raw[rows].rearrange("p e i -> p (e i)").bitcast(I32), 0)
+        nc.gpsimd.memset(s2_t[:].rearrange("p e i -> p (e i)").bitcast(I32), 0)
         nc.gpsimd.memset(s1_t[:].rearrange("p e i -> p (e i)").bitcast(I32), 0)
 
         dyT_rows = dyT.rearrange("(p t) n -> p t n", t=PACK)
@@ -73,41 +77,49 @@ def tile_moe_bdx_mlp_relu_kernel(
                 w2_words[2 * q : 2 * q + 2].rearrange("e g p b -> p (e g) b").bitcast(I32),
             )
 
-        def load_w1(q):
+        def as_i32(view):
+            e = view.shape[1]
+            return view.rearrange("p e i -> p (e i)").bitcast(I32).rearrange("p (e i) -> p e i", e=e)
+
+        for j in range(2):
             nc.sync.dma_start(
-                w1_t[q][:].rearrange("p e b -> p (e b)").bitcast(I32).rearrange("p (e b) -> p e b", e=2),
-                w1_words[2 * q : 2 * q + 2].rearrange("e g p b -> p (e g) b").bitcast(I32),
+                as_i32(s2_raw[16 * j : 16 * j + 16]),
+                w2_scales[4 * j : 4 * j + 4].rearrange("e g f i -> (g f) e i").bitcast(I32),
             )
-
-        def load_scales(tile, scales):
-            for quad in range(4):
-                nc.sync.dma_start(
-                    tile[32 * quad : 32 * quad + 4].rearrange("p e i -> p (e i)").bitcast(I32).rearrange("p (e i) -> p e i", e=E),
-                    scales[:, :, 4 * quad : 4 * quad + 4, :].rearrange("e g f i -> f (e g) i").bitcast(I32),
-                )
-
+        nc.vector.tensor_copy(
+            s2_mid[:].rearrange("p e (t m) -> p e t m", t=PACK), s2_raw[:].rearrange("p e (m t) -> p e t m", t=PACK)
+        )
         nc.sync.dma_start(offs_t[:], offs)
         load_gate(0)
         for t in range(PACK):
             nc.sync.dma_start(dy[t][:], dyT_rows[:, t, :])
-        load_scales(s2_raw, w2_scales)
         load_w2(0)
-        load_pre(0)
         load_gate(1)
-        load_scales(s1_t, w1_scales)
-        load_w1(0)
-        for q in range(1, PIECES):
-            load_w2(q)
-            load_pre(q)
-            load_w1(q)
-            if q + 1 < PIECES:
-                load_gate(q + 1)
+        load_pre(0)
+        for j in range(2):
+            for quad in range(4):
+                nc.sync.dma_start(
+                    as_i32(s2_t[32 * quad : 32 * quad + 4, 4 * j : 4 * j + 4, :]),
+                    as_i32(s2_mid[16 * j + 4 * quad : 16 * j + 4 * quad + 4]),
+                )
+        load_pre(1)
+        load_gate(2)
+        load_w2(1)
+        for quad in range(4):
+            nc.sync.dma_start(
+                as_i32(s1_t[32 * quad : 32 * quad + 4]),
+                w1_scales[:, :, 4 * quad : 4 * quad + 4, :].rearrange("e g f k -> f (e g) k").bitcast(I32),
+            )
+        nc.sync.dma_start(as_i32(w1_t[:]), w1_words.rearrange("e g p b -> p (e g) b").bitcast(I32))
+        load_w2(2)
+        load_gate(3)
+        load_pre(2)
+        load_w2(3)
+        load_pre(3)
         nc.sync.dma_start(pos1_t[:], pos1)
         nc.sync.dma_start(pos2_t[:], pos2)
 
-        g4 = {}
-        codes = {}
-        signs = {}
+        g4, grouped, signs, ones, codes, das = {}, {}, {}, {}, {}, {}
 
         def gather(q, t):
             if t == 0:
@@ -119,103 +131,153 @@ def tile_moe_bdx_mlp_relu_kernel(
                 MULT,
             )
 
-        def permute(q):
+        def permute_words(q):
             nc.vector.tensor_copy(
                 w2_t[q][:].rearrange("p e b -> p (e b)").bitcast(U16).rearrange("p (e t m) -> p e t m", e=2, t=PACK),
                 w2_raw[q][:].rearrange("p e b -> p (e b)").bitcast(U16).rearrange("p (e m t) -> p e t m", e=2, t=PACK),
             )
-            nc.vector.tensor_copy(
-                s2_t[q][:].rearrange("p e (t m) -> p e t m", t=PACK),
-                s2_raw[:, 2 * q : 2 * q + 2, :].rearrange("p e (m t) -> p e t m", t=PACK),
+
+        def interleave(q):
+            grouped[q] = work.tile([P, PIECE, PACK], BF16, name="gb", align_bytes=64)
+            for h in range(2):
+                cols = slice(h * C, (h + 1) * C)
+                nc.scalar.copy(
+                    grouped[q][:, cols, :].rearrange("p (c i) t -> p c t i", i=4),
+                    g4[q][:, :, cols].rearrange("p t (c i) -> p c t i", i=4),
+                )
+
+        def sign(q):
+            signs[q] = work.tile([P, PIECE, PACK], BF16, name="sg")
+            nc.scalar.activation(
+                signs[q][:].rearrange("p (c i) t -> p c t i", i=4),
+                pre[q][:].rearrange("p t (c i) -> p c t i", i=4),
+                SIGN,
             )
 
-        def interleave(e):
-            q, h = divmod(e, 2)
-            gb = work.tile([P, C, PACK], BF16, name="gb", align_bytes=64)
-            nc.scalar.copy(gb[:], g4[q][:, :, h * C : (h + 1) * C].rearrange("p t s -> p s t"))
-            return gb
+        def mask(q):
+            ones[q] = work.tile([P, PIECE, PACK], BF16, name="mk")
+            if q == 0:
+                nc.scalar.activation(ones[q][:], signs[q][:], RELU)
+            else:
+                nc.vector.tensor_scalar(ones[q][:], signs[q][:], 0.0, None, MAX)
 
-        def sign(e):
-            q, h = divmod(e, 2)
-            sg = work.tile([P, C, PACK], BF16, name="sg")
-            nc.scalar.activation(sg[:], pre[q][:, :, h * C : (h + 1) * C].rearrange("p t s -> p s t"), SIGN)
-            signs[e] = sg
-
-        def quantise_g(e):
-            words = work.tile([P, C], U32, name="g_words", align_bytes=64)
-            scales = work.tile([P, C], U8, name="g_scales", align_bytes=64)
+        def quantise_g(q, first, width):
+            if first == 0:
+                codes[q] = (
+                    work.tile([P, PIECE], U32, name="g_words", align_bytes=64),
+                    work.tile([P, PIECE], U8, name="g_scales", align_bytes=64),
+                )
+                das[q] = work.tile([P, PIECE, PACK], BF16, name="da", align_bytes=64)
+            cols = slice(first, first + width)
             nc.vector.quantize_mx(
-                out=words[:].bitcast(FP8X4), scales=scales[:], in_=grouped[e][:].rearrange("p s t -> p (s t)")
+                out=codes[q][0][:, cols].bitcast(FP8X4),
+                scales=codes[q][1][:, cols],
+                in_=grouped[q][:, cols, :].rearrange("p s t -> p (s t)"),
             )
-            codes[e] = words, scales
 
-        def first_product(e, c):
-            q, h = divmod(e, 2)
-            words, scales = codes[e]
-            if c == 0:
-                das[e] = work.tile([P, C, PACK], BF16, name="da", align_bytes=64)
+        def first_product(q, c):
+            h = c * CHUNK // C
             cols = slice(c * CHUNK, (c + 1) * CHUNK)
             bank = psum1.tile([P, PACK, CHUNK], F32, name="bank")
             for t in range(PACK):
                 nc.tensor.matmul_mx(
                     out=bank[:, t, :],
                     lhsT=w2_t[q][:, h, t * 2 * P : (t + 1) * 2 * P].bitcast(FP4X4),
-                    lhsT_scale=s2_t[q][:, h, t * P : (t + 1) * P],
-                    rhs=words[:, cols].bitcast(FP8X4),
-                    rhs_scale=scales[:, cols],
+                    lhsT_scale=s2_t[:, 2 * q + h, t * P : (t + 1) * P],
+                    rhs=codes[q][0][:, cols].bitcast(FP8X4),
+                    rhs_scale=codes[q][1][:, cols],
                     start=True,
                     stop=True,
                 )
-            nc.vector.scalar_tensor_tensor(
-                das[e][:, cols, :], signs[e][:, cols, :], 0.0, bank[:].rearrange("p t s -> p s t"), MAX, MULT
-            )
+            return cols, bank[:].rearrange("p t s -> p s t")
 
-        def second_product(e, first, width):
-            q, h = divmod(e, 2)
-            words = work.tile([P, C], U32, name="da_words", align_bytes=64)
-            scales = work.tile([P, C], U8, name="da_scales", align_bytes=64)
+        def product_by_mask(q, h):
+            raw = work.tile([P, C, PACK], BF16, name="raw")
+            for c in range(2):
+                cols, bank = first_product(q, 2 * h + c)
+                nc.scalar.copy(raw[:, c * CHUNK : (c + 1) * CHUNK, :], bank)
+            cols = slice(h * C, (h + 1) * C)
+            nc.vector.tensor_tensor(das[q][:, cols, :], raw[:], ones[q][:, cols, :], MULT)
+
+        def product_by_sign(q, c):
+            cols, bank = first_product(q, c)
+            nc.vector.scalar_tensor_tensor(das[q][:, cols, :], signs[q][:, cols, :], 0.0, bank, MAX, MULT)
+
+        def second_product(q, first, width):
+            words = work.tile([P, PIECE], U32, name="da_words", align_bytes=64)
+            scales = work.tile([P, PIECE], U8, name="da_scales", align_bytes=64)
             nc.vector.quantize_mx(
                 out=words[:, 0:width].bitcast(FP8X4),
                 scales=scales[:, 0:width],
-                in_=das[e][:, first : first + width, :].rearrange("p s t -> p (s t)"),
+                in_=das[q][:, first : first + width, :].rearrange("p s t -> p (s t)"),
             )
             for k in range(2):
-                acc = psum2.tile([P, C], F32, name=f"acc{k}")
-                nc.tensor.matmul_mx(
-                    out=acc[:, 0:width],
-                    lhsT=w1_t[q][:, h, k * 2 * P : (k + 1) * 2 * P].bitcast(FP4X4),
-                    lhsT_scale=s1_t[:, e, k * P : (k + 1) * P],
-                    rhs=words[:, 0:width].bitcast(FP8X4),
-                    rhs_scale=scales[:, 0:width],
-                    start=True,
-                    stop=True,
-                )
-                nc.scalar.copy(dx[k][:, e * C + first : e * C + first + width], acc[:, 0:width])
+                acc = psum2.tile([P, PIECE], F32, name=f"acc{k}")
+                for start in range(0, width, min(width, C)):
+                    span = slice(start, start + min(width, C))
+                    h = (first + start) // C
+                    nc.tensor.matmul_mx(
+                        out=acc[:, span],
+                        lhsT=w1_t[:, 2 * q + h, k * 2 * P : (k + 1) * 2 * P].bitcast(FP4X4),
+                        lhsT_scale=s1_t[:, 2 * q + h, k * P : (k + 1) * P],
+                        rhs=words[:, span].bitcast(FP8X4),
+                        rhs_scale=scales[:, span],
+                        start=True,
+                        stop=True,
+                    )
+                slots = slice(q * PIECE + first, q * PIECE + first + width)
+                if k == 0 and first + width == PIECE and q == PIECES - 1:
+                    nc.vector.tensor_copy(dx[k][:, slots], acc[:, 0:width])
+                else:
+                    nc.scalar.copy(dx[k][:, slots], acc[:, 0:width])
 
-        grouped = {}
-        das = {}
-
-        def fetch(q):
+        for q in range(2):
             for t in range(PACK):
                 gather(q, t)
-            for e in (2 * q, 2 * q + 1):
-                grouped[e] = interleave(e)
-                sign(e)
-
-        fetch(0)
-        permute(0)
-        for q in range(PIECES):
-            if q + 1 < PIECES:
-                fetch(q + 1)
-                permute(q + 1)
-            for e in (2 * q, 2 * q + 1):
-                quantise_g(e)
-                first_product(e, 0)
-                if e > 0:
-                    second_product(e - 1, 0, C)
-                first_product(e, 1)
-        second_product(E - 1, 0, CHUNK)
-        second_product(E - 1, CHUNK, CHUNK)
+            interleave(q)
+            permute_words(q)
+            if q == 0:
+                sign(0)
+        quantise_g(0, 0, PIECE)
+        mask(0)
+        gather(2, 0)
+        gather(2, 1)
+        product_by_mask(0, 0)
+        gather(2, 2)
+        product_by_mask(0, 1)
+        quantise_g(1, 0, PIECE)
+        sign(1)
+        gather(2, 3)
+        interleave(2)
+        second_product(0, 0, PIECE)
+        mask(1)
+        gather(3, 0)
+        product_by_mask(1, 0)
+        gather(3, 1)
+        permute_words(2)
+        product_by_mask(1, 1)
+        gather(3, 2)
+        sign(2)
+        quantise_g(2, 0, PIECE)
+        gather(3, 3)
+        interleave(3)
+        second_product(1, 0, PIECE)
+        sign(3)
+        product_by_sign(2, 0)
+        product_by_sign(2, 1)
+        quantise_g(3, 0, C)
+        product_by_sign(2, 2)
+        product_by_sign(2, 3)
+        quantise_g(3, C, C)
+        permute_words(3)
+        product_by_sign(3, 0)
+        second_product(2, 0, PIECE)
+        product_by_sign(3, 1)
+        product_by_sign(3, 2)
+        second_product(3, 0, C)
+        product_by_sign(3, 3)
+        second_product(3, C, CHUNK)
+        second_product(3, C + CHUNK, CHUNK)
 
         for k in range(2):
             part1 = keep.tile([P, T], F32, name=f"part1_{k}")

@@ -27,7 +27,7 @@ BYTES = 4 * N * T + 4 * H * S + E * (N * H + H * K) * 17 // 32 + 4 * S + 2 * S +
 PIECE = 512
 PIECES = S // PIECE
 CHUNK = 128
-SHARES = (((0, 512, "gpsimd"), (512, 512, "gpsimd")), ((0, 512, "gpsimd"), (512, 256, "gpsimd"), (768, 256, "vector")))
+SHARES = (((0, 512, "gpsimd"), (512, 512, "gpsimd")), ((0, 512, "gpsimd"), (512, 256, "vector"), (768, 256, "vector")))
 
 
 def tile_moe_bdx_mlp_relu_kernel(
@@ -81,11 +81,19 @@ def tile_moe_bdx_mlp_relu_kernel(
             e = view.shape[1]
             return view.rearrange("p e i -> p (e i)").bitcast(I32).rearrange("p (e i) -> p e i", e=e)
 
+        def move_scales(j):
+            for quad in range(4):
+                nc.sync.dma_start(
+                    as_i32(s2_t[32 * quad : 32 * quad + 4, 4 * j : 4 * j + 4, :]),
+                    as_i32(s2_mid[16 * j + 4 * quad : 16 * j + 4 * quad + 4]),
+                )
+
         for j in range(2):
             nc.sync.dma_start(
                 as_i32(s2_raw[16 * j : 16 * j + 16]),
                 w2_scales[4 * j : 4 * j + 4].rearrange("e g f i -> (g f) e i").bitcast(I32),
             )
+        load_w2(0)
         nc.vector.tensor_copy(
             s2_mid[:].rearrange("p e (t m) -> p e t m", t=PACK), s2_raw[:].rearrange("p e (m t) -> p e t m", t=PACK)
         )
@@ -93,27 +101,22 @@ def tile_moe_bdx_mlp_relu_kernel(
         load_gate(0)
         for t in range(PACK):
             nc.sync.dma_start(dy[t][:], dyT_rows[:, t, :])
-        load_w2(0)
         load_gate(1)
         load_pre(0)
-        for j in range(2):
-            for quad in range(4):
-                nc.sync.dma_start(
-                    as_i32(s2_t[32 * quad : 32 * quad + 4, 4 * j : 4 * j + 4, :]),
-                    as_i32(s2_mid[16 * j + 4 * quad : 16 * j + 4 * quad + 4]),
-                )
-        load_pre(1)
+        move_scales(0)
         load_gate(2)
+        load_pre(1)
         load_w2(1)
+        nc.sync.dma_start(as_i32(w1_t[:]), w1_words.rearrange("e g p b -> p (e g) b").bitcast(I32))
         for quad in range(4):
             nc.sync.dma_start(
                 as_i32(s1_t[32 * quad : 32 * quad + 4]),
                 w1_scales[:, :, 4 * quad : 4 * quad + 4, :].rearrange("e g f k -> f (e g) k").bitcast(I32),
             )
-        nc.sync.dma_start(as_i32(w1_t[:]), w1_words.rearrange("e g p b -> p (e g) b").bitcast(I32))
-        load_w2(2)
         load_gate(3)
         load_pre(2)
+        load_w2(2)
+        move_scales(1)
         load_w2(3)
         load_pre(3)
         nc.sync.dma_start(pos1_t[:], pos1)
@@ -231,11 +234,11 @@ def tile_moe_bdx_mlp_relu_kernel(
                 else:
                     nc.scalar.copy(dx[k][:, slots], acc[:, 0:width])
 
+        permute_words(0)
         for q in range(2):
             for t in range(PACK):
                 gather(q, t)
             interleave(q)
-            permute_words(q)
             if q == 0:
                 sign(0)
         quantise_g(0, 0, PIECE)
@@ -249,6 +252,7 @@ def tile_moe_bdx_mlp_relu_kernel(
         sign(1)
         gather(2, 3)
         interleave(2)
+        permute_words(1)
         second_product(0, 0, PIECE)
         mask(1)
         gather(3, 0)

@@ -27,7 +27,7 @@ BYTES = 4 * N * T + 4 * H * S + E * (N * H + H * K) * 17 // 32 + 4 * S + 2 * S +
 PIECE = 512
 PIECES = S // PIECE
 CHUNK = 128
-SHARES = (((0, 512, "gpsimd"), (512, 512, "gpsimd")), ((0, 512, "gpsimd"), (512, 256, "vector"), (768, 256, "vector")))
+SHARES = (((0, 1024, "gpsimd"),), ((0, 512, "gpsimd"), (512, 256, "vector"), (768, 256, "vector")))
 
 
 def tile_moe_bdx_mlp_relu_kernel(
@@ -122,7 +122,7 @@ def tile_moe_bdx_mlp_relu_kernel(
         nc.sync.dma_start(pos1_t[:], pos1)
         nc.sync.dma_start(pos2_t[:], pos2)
 
-        g4, grouped, signs, ones, codes, das = {}, {}, {}, {}, {}, {}
+        g4, grouped, signs, ones, codes, raws, das = {}, {}, {}, {}, {}, {}, {}
 
         def gather(q, t):
             if t == 0:
@@ -142,8 +142,9 @@ def tile_moe_bdx_mlp_relu_kernel(
 
         def interleave(q):
             grouped[q] = work.tile([P, PIECE, PACK], BF16, name="gb", align_bytes=64)
-            for h in range(2):
-                cols = slice(h * C, (h + 1) * C)
+            step = C if q == PIECES - 1 else PIECE
+            for first in range(0, PIECE, step):
+                cols = slice(first, first + step)
                 nc.scalar.copy(
                     grouped[q][:, cols, :].rearrange("p (c i) t -> p c t i", i=4),
                     g4[q][:, :, cols].rearrange("p t (c i) -> p c t i", i=4),
@@ -194,13 +195,13 @@ def tile_moe_bdx_mlp_relu_kernel(
                 )
             return cols, bank[:].rearrange("p t s -> p s t")
 
-        def product_by_mask(q, h):
-            raw = work.tile([P, C, PACK], BF16, name="raw")
-            for c in range(2):
-                cols, bank = first_product(q, 2 * h + c)
-                nc.scalar.copy(raw[:, c * CHUNK : (c + 1) * CHUNK, :], bank)
-            cols = slice(h * C, (h + 1) * C)
-            nc.vector.tensor_tensor(das[q][:, cols, :], raw[:], ones[q][:, cols, :], MULT)
+        def product_by_mask(q, c):
+            if c == 0:
+                raws[q] = work.tile([P, PIECE, PACK], BF16, name="raw")
+            cols, bank = first_product(q, c)
+            nc.scalar.copy(raws[q][:, cols, :], bank)
+            if c == PIECE // CHUNK - 1:
+                nc.vector.tensor_tensor(das[q][:], raws[q][:], ones[q][:], MULT)
 
         def product_by_sign(q, c):
             cols, bank = first_product(q, c)
@@ -246,8 +247,10 @@ def tile_moe_bdx_mlp_relu_kernel(
         gather(2, 0)
         gather(2, 1)
         product_by_mask(0, 0)
-        gather(2, 2)
         product_by_mask(0, 1)
+        gather(2, 2)
+        product_by_mask(0, 2)
+        product_by_mask(0, 3)
         quantise_g(1, 0, PIECE)
         sign(1)
         gather(2, 3)
@@ -257,9 +260,11 @@ def tile_moe_bdx_mlp_relu_kernel(
         mask(1)
         gather(3, 0)
         product_by_mask(1, 0)
+        product_by_mask(1, 1)
         gather(3, 1)
         permute_words(2)
-        product_by_mask(1, 1)
+        product_by_mask(1, 2)
+        product_by_mask(1, 3)
         gather(3, 2)
         sign(2)
         quantise_g(2, 0, PIECE)

from contextlib import ExitStack

import concourse.mybir as mybir

K, T, E, C, H, N = 256, 1024, 8, 256, 512, 512
S = E * C
P = 128
PACK = 4

F32 = mybir.dt.float32
BF16 = mybir.dt.bfloat16
I32 = mybir.dt.int32
U32 = mybir.dt.uint32
U16 = mybir.dt.uint16
U8 = mybir.dt.uint8
FP8X4 = mybir.dt.float8_e4m3fn_x4
FP4X4 = mybir.dt.float4_e2m1fn_x4
MULT = mybir.AluOpType.mult
ADD = mybir.AluOpType.add
MAX = mybir.AluOpType.max
SIGN = mybir.ActivationFunctionType.Sign
RELU = mybir.ActivationFunctionType.Relu

FLOPS = 2 * S * (N * H + H * K)
BYTES = 4 * N * T + 4 * H * S + E * (N * H + H * K) * 17 // 32 + 4 * S + 2 * S + 2 * 2 * T + 4 * K * T

PIECE = 512
PIECES = S // PIECE
CHUNK = 128
SHARES = (((0, 1024, "gpsimd"),), ((0, 512, "gpsimd"), (512, 256, "vector"), (768, 256, "vector")))


def tile_moe_bdx_mlp_relu_kernel(
    tc, dyT, a, w2_words, w2_scales, w1_words, w1_scales, gate, offs, pos1, pos2, out
):
    nc = tc.nc
    with ExitStack() as ctx:
        lists = ctx.enter_context(tc.tile_pool(name="lists", bufs=1))
        keep = ctx.enter_context(tc.tile_pool(name="keep", bufs=1))
        work = ctx.enter_context(tc.tile_pool(name="work", bufs=3))
        psum1 = ctx.enter_context(tc.psum_pool(name="psum1", bufs=4))
        psum2 = ctx.enter_context(tc.psum_pool(name="psum2", bufs=2))

        offs_t = lists.tile([P, S // 16], U16, name="offs_t")
        pos1_t = lists.tile([P, T // 16], U16, name="pos1_t")
        pos2_t = lists.tile([P, T // 16], U16, name="pos2_t")

        dy = [keep.tile([P, T], F32, name=f"dy{t}") for t in range(PACK)]
        gates = [keep.tile([P, PIECE], F32, name=f"gates{q}") for q in range(PIECES)]
        pre = [keep.tile([P, PACK, PIECE], F32, name=f"pre{q}") for q in range(PIECES)]
        w2_raw = [keep.tile([P, 2, 2 * H], U8, name=f"w2_raw{q}") for q in range(PIECES)]
        w2_t = [keep.tile([P, 2, 2 * H], U8, name=f"w2_t{q}", align_bytes=64) for q in range(PIECES)]
        s2_raw = keep.tile([P, E // 2, H], U8, name="s2_raw")
        s2_mid = keep.tile([P, E // 2, H], U8, name="s2_mid")
        s2_t = keep.tile([P, E, H], U8, name="s2_t", align_bytes=64)
        w1_t = keep.tile([P, E, 2 * K], U8, name="w1_t", align_bytes=64)
        s1_t = keep.tile([P, E, K], U8, name="s1_t", align_bytes=64)
        dx = [keep.tile([P, S], F32, name=f"dx{k}") for k in range(2)]

        for rows in (slice(32, 64), slice(64, P)):
            nc.gpsimd.memset(s2_raw[rows].rearrange("p e i -> p (e i)").bitcast(I32), 0)
        nc.gpsimd.memset(s2_t[:].rearrange("p e i -> p (e i)").bitcast(I32), 0)
        nc.gpsimd.memset(s1_t[:].rearrange("p e i -> p (e i)").bitcast(I32), 0)

        dyT_rows = dyT.rearrange("(p t) n -> p t n", t=PACK)
        a_rows = a.rearrange("(p t) s -> p t s", t=PACK)

        def load_gate(q):
            nc.sync.dma_start(gates[q][:], gate[0:P, q * PIECE : (q + 1) * PIECE])

        def load_pre(q):
            nc.sync.dma_start(pre[q][:], a_rows[:, :, q * PIECE : (q + 1) * PIECE])

        def load_w2(q):
            nc.sync.dma_start(
                w2_raw[q][:].rearrange("p e b -> p (e b)").bitcast(I32).rearrange("p (e b) -> p e b", e=2),
                w2_words[2 * q : 2 * q + 2].rearrange("e g p b -> p (e g) b").bitcast(I32),
            )

        def as_i32(view):
            e = view.shape[1]
            return view.rearrange("p e i -> p (e i)").bitcast(I32).rearrange("p (e i) -> p e i", e=e)

        def move_scales(j):
            for quad in range(4):
                nc.sync.dma_start(
                    as_i32(s2_t[32 * quad : 32 * quad + 4, 4 * j : 4 * j + 4, :]),
                    as_i32(s2_mid[16 * j + 4 * quad : 16 * j + 4 * quad + 4]),
                )

        for j in range(2):
            nc.sync.dma_start(
                as_i32(s2_raw[16 * j : 16 * j + 16]),
                w2_scales[4 * j : 4 * j + 4].rearrange("e g f i -> (g f) e i").bitcast(I32),
            )
        load_w2(0)
        nc.vector.tensor_copy(
            s2_mid[:].rearrange("p e (t m) -> p e t m", t=PACK), s2_raw[:].rearrange("p e (m t) -> p e t m", t=PACK)
        )
        nc.sync.dma_start(offs_t[:], offs)
        load_gate(0)
        for t in range(PACK):
            nc.sync.dma_start(dy[t][:], dyT_rows[:, t, :])
        load_gate(1)
        load_pre(0)
        move_scales(0)
        load_gate(2)
        load_pre(1)
        load_w2(1)
        nc.sync.dma_start(as_i32(w1_t[:]), w1_words.rearrange("e g p b -> p (e g) b").bitcast(I32))
        for quad in range(4):
            nc.sync.dma_start(
                as_i32(s1_t[32 * quad : 32 * quad + 4]),
                w1_scales[:, :, 4 * quad : 4 * quad + 4, :].rearrange("e g f k -> f (e g) k").bitcast(I32),
            )
        load_gate(3)
        load_pre(2)
        load_w2(2)
        move_scales(1)
        load_w2(3)
        load_pre(3)
        nc.sync.dma_start(pos1_t[:], pos1)
        nc.sync.dma_start(pos2_t[:], pos2)

        g4, grouped, signs, ones, codes, raws, das = {}, {}, {}, {}, {}, {}, {}

        def gather(q, t):
            if t == 0:
                g4[q] = work.tile([P, PACK, PIECE], F32, name="g4")
            nc.vector.tensor_tensor(
                g4[q][:, t, :],
                dy[t][:].indirect(offs_t[:, q * (PIECE // 16) : (q + 1) * (PIECE // 16)]),
                gates[q][:],
                MULT,
            )

        def permute_words(q):
            nc.vector.tensor_copy(
                w2_t[q][:].rearrange("p e b -> p (e b)").bitcast(U16).rearrange("p (e t m) -> p e t m", e=2, t=PACK),
                w2_raw[q][:].rearrange("p e b -> p (e b)").bitcast(U16).rearrange("p (e m t) -> p e t m", e=2, t=PACK),
            )

        def interleave(q):
            grouped[q] = work.tile([P, PIECE, PACK], BF16, name="gb", align_bytes=64)
            step = C if q == PIECES - 1 else PIECE
            for first in range(0, PIECE, step):
                cols = slice(first, first + step)
                nc.scalar.copy(
                    grouped[q][:, cols, :].rearrange("p (c i) t -> p c t i", i=4),
                    g4[q][:, :, cols].rearrange("p t (c i) -> p c t i", i=4),
                )

        def sign(q):
            signs[q] = work.tile([P, PIECE, PACK], BF16, name="sg")
            nc.scalar.activation(
                signs[q][:].rearrange("p (c i) t -> p c t i", i=4),
                pre[q][:].rearrange("p t (c i) -> p c t i", i=4),
                SIGN,
            )

        def mask(q):
            ones[q] = work.tile([P, PIECE, PACK], BF16, name="mk")
            if q == 0:
                nc.scalar.activation(ones[q][:], signs[q][:], RELU)
            else:
                nc.vector.tensor_scalar(ones[q][:], signs[q][:], 0.0, None, MAX)

        def quantise_g(q, first, width):
            if first == 0:
                codes[q] = (
                    work.tile([P, PIECE], U32, name="g_words", align_bytes=64),
                    work.tile([P, PIECE], U8, name="g_scales", align_bytes=64),
                )
                das[q] = work.tile([P, PIECE, PACK], BF16, name="da", align_bytes=64)
            cols = slice(first, first + width)
            nc.vector.quantize_mx(
                out=codes[q][0][:, cols].bitcast(FP8X4),
                scales=codes[q][1][:, cols],
                in_=grouped[q][:, cols, :].rearrange("p s t -> p (s t)"),
            )

        def first_product(q, c):
            h = c * CHUNK // C
            cols = slice(c * CHUNK, (c + 1) * CHUNK)
            bank = psum1.tile([P, PACK, CHUNK], F32, name="bank")
            for t in range(PACK):
                nc.tensor.matmul_mx(
                    out=bank[:, t, :],
                    lhsT=w2_t[q][:, h, t * 2 * P : (t + 1) * 2 * P].bitcast(FP4X4),
                    lhsT_scale=s2_t[:, 2 * q + h, t * P : (t + 1) * P],
                    rhs=codes[q][0][:, cols].bitcast(FP8X4),
                    rhs_scale=codes[q][1][:, cols],
                    start=True,
                    stop=True,
                )
            return cols, bank[:].rearrange("p t s -> p s t")

        def product_by_mask(q, c):
            if c == 0:
                raws[q] = work.tile([P, PIECE, PACK], BF16, name="raw")
            cols, bank = first_product(q, c)
            nc.scalar.copy(raws[q][:, cols, :], bank)
            if c == PIECE // CHUNK - 1:
                nc.vector.tensor_tensor(das[q][:], raws[q][:], ones[q][:], MULT)

        def product_by_sign(q, c):
            cols, bank = first_product(q, c)
            nc.vector.scalar_tensor_tensor(das[q][:, cols, :], signs[q][:, cols, :], 0.0, bank, MAX, MULT)

        def second_product(q, first, width):
            words = work.tile([P, PIECE], U32, name="da_words", align_bytes=64)
            scales = work.tile([P, PIECE], U8, name="da_scales", align_bytes=64)
            nc.vector.quantize_mx(
                out=words[:, 0:width].bitcast(FP8X4),
                scales=scales[:, 0:width],
                in_=das[q][:, first : first + width, :].rearrange("p s t -> p (s t)"),
            )
            for k in range(2):
                acc = psum2.tile([P, PIECE], F32, name=f"acc{k}")
                for start in range(0, width, min(width, C)):
                    span = slice(start, start + min(width, C))
                    h = (first + start) // C
                    nc.tensor.matmul_mx(
                        out=acc[:, span],
                        lhsT=w1_t[:, 2 * q + h, k * 2 * P : (k + 1) * 2 * P].bitcast(FP4X4),
                        lhsT_scale=s1_t[:, 2 * q + h, k * P : (k + 1) * P],
                        rhs=words[:, span].bitcast(FP8X4),
                        rhs_scale=scales[:, span],
                        start=True,
                        stop=True,
                    )
                slots = slice(q * PIECE + first, q * PIECE + first + width)
                if k == 0 and first + width == PIECE and q == PIECES - 1:
                    nc.vector.tensor_copy(dx[k][:, slots], acc[:, 0:width])
                else:
                    nc.scalar.copy(dx[k][:, slots], acc[:, 0:width])

        permute_words(0)
        for q in range(2):
            for t in range(PACK):
                gather(q, t)
            interleave(q)
            if q == 0:
                sign(0)
        quantise_g(0, 0, PIECE)
        mask(0)
        gather(2, 0)
        gather(2, 1)
        product_by_mask(0, 0)
        product_by_mask(0, 1)
        gather(2, 2)
        product_by_mask(0, 2)
        product_by_mask(0, 3)
        quantise_g(1, 0, PIECE)
        sign(1)
        gather(2, 3)
        interleave(2)
        permute_words(1)
        second_product(0, 0, PIECE)
        mask(1)
        gather(3, 0)
        product_by_mask(1, 0)
        product_by_mask(1, 1)
        gather(3, 1)
        permute_words(2)
        product_by_mask(1, 2)
        product_by_mask(1, 3)
        gather(3, 2)
        sign(2)
        quantise_g(2, 0, PIECE)
        gather(3, 3)
        interleave(3)
        second_product(1, 0, PIECE)
        sign(3)
        product_by_sign(2, 0)
        product_by_sign(2, 1)
        quantise_g(3, 0, C)
        product_by_sign(2, 2)
        product_by_sign(2, 3)
        quantise_g(3, C, C)
        permute_words(3)
        product_by_sign(3, 0)
        second_product(2, 0, PIECE)
        product_by_sign(3, 1)
        product_by_sign(3, 2)
        second_product(3, 0, C)
        product_by_sign(3, 3)
        second_product(3, C, CHUNK)
        second_product(3, C + CHUNK, CHUNK)

        for k in range(2):
            part1 = keep.tile([P, T], F32, name=f"part1_{k}")
            nc.vector.tensor_copy(part1[:], dx[k][:].indirect(pos1_t[:]))
            for first, width, adder in SHARES[k]:
                part2 = keep.tile([P, width], F32, name=f"part2_{k}_{first}")
                total = keep.tile([P, width], F32, name=f"total_{k}_{first}")
                nc.vector.tensor_copy(part2[:], dx[k][:].indirect(pos2_t[:, first // 16 : (first + width) // 16]))
                engine = nc.vector if adder == "vector" else nc.gpsimd
                engine.tensor_tensor(total[:], part1[:, first : first + width], part2[:], ADD)
                nc.sync.dma_start(out[k * P : (k + 1) * P, first : first + width], total[:])
